import numpy as np, ml_dtypes
CORES = [78,86,94,102,110,118]
N = 6
NB, TK, FT = 4, 32, 4
def setup_inputs(rng):
    return {"x": rng.standard_normal((N, NB, 128, TK), dtype=np.float32).astype(ml_dtypes.bfloat16), "w1": (rng.standard_normal((N, 128, FT * 128), dtype=np.float32) / 8).astype(ml_dtypes.bfloat16), "w2": (rng.standard_normal((N, 128, FT * 128), dtype=np.float32) / np.float32(8 * np.sqrt(FT))).astype(ml_dtypes.bfloat16)}
def setup_inputs_big(rng):
    d = setup_inputs(rng)
    for k in ("x",): d[k] = (d[k].astype(np.float32) * 1048576.0).astype(d[k].dtype)
    return d
def setup_inputs_small(rng):
    d = setup_inputs(rng)
    for k in ("x",): d[k] = (d[k].astype(np.float32) * (1 / 1048576.0)).astype(d[k].dtype)
    return d
def reference(x, w1, w2):
    W1, W2 = w1.astype(np.float64), w2.astype(np.float64)
    a = x[0].astype(np.float64)
    for s in range(N):
        a = sum(np.einsum("kf,bkn->bfn", W2[s][:, 128 * f:128 * f + 128], np.maximum(np.einsum("kf,bkn->bfn", W1[s][:, 128 * f:128 * f + 128], a), 0.0)) for f in range(FT))
    y = np.full(x.shape, np.nan, ml_dtypes.bfloat16)
    y[N - 1] = a.astype(ml_dtypes.bfloat16)
    return {"y": y}

@@ -1,0 +1,146 @@
+from concourse.mybir import AluOpType
+
+N, NB, TK, FT, P = 6, 4, 32, 4, 128
+HOST = [0, 1, 1, 5, 5, 5]
+NCH = 2
+COLS = NB * TK
+CW = COLS // NCH
+BPC = NB // NCH
+WC = 2 * FT * P
+MAXST = max(HOST.count(r) for r in range(N))
+NZ, NA = 6, 2
+ACT_ENG = 8
+W_ENG = 8
+
+SCRATCH = {
+    "wts": ("sbuf", [P, MAXST * WC], "bfloat16"),
+    "ain": ("sbuf", [P, COLS], "bfloat16"),
+    "aout": ("sbuf", [P, MAXST * COLS], "bfloat16"),
+    "hid": ("sbuf", [P, MAXST * NCH * FT * CW], "bfloat16"),
+    "zero": ("sbuf", [P, CW], "float32"),
+}
+for _i in range(NZ):
+    SCRATCH["z%d" % _i] = ("psum", [P, 512], "float32")
+for _i in range(NA):
+    SCRATCH["p%d" % _i] = ("psum", [P, 512], "float32")
+
+SEMAPHORES = (["wl1", "wl2", "zs", "tdone", "vdone", "sent"]
+              + ["arr%d" % c for c in range(NCH)] + ["wr%d" % j for j in range(MAXST)]
+              + ["st%d" % b for b in range(BPC)])
+
+
+def _engines(topo, src, dst, n):
+    full, m, b, k = topo.mask(src, dst), 0, 0, 0
+    while k < n:
+        if (full >> b) & 1:
+            m |= 1 << b
+            k += 1
+        b += 1
+    return m
+
+
+def rank_program(g, core, T, topo):
+    rank = T.rank_of(core)
+    if rank is None:
+        return
+    sem = T.sem
+    te, ve = g.tensor, g.vector
+    ldq = [g.sync, g.scalar]
+    mine = [s for s in range(N) if HOST[s] == rank]
+    slot = (rank - mine[0]) if mine else 0
+
+    def load_x(c):
+        for b in range(BPC):
+            m = c * BPC + b
+            ldq[b % 2].dma_start(T.ain[:, m * TK:(m + 1) * TK], T.x[m]).then_inc(sem["arr%d" % c], 16)
+
+    if rank == 0:
+        load_x(0)
+    g.sync.dma_start(T.wts[:, slot * WC:slot * WC + FT * P], T.w1[:, :]).then_inc(sem.wl1, 16)
+    g.scalar.dma_start(T.wts[:, slot * WC + FT * P:(slot + 1) * WC], T.w2[:, :]).then_inc(sem.wl2, 16)
+    if rank == 0:
+        for c in range(1, NCH):
+            load_x(c)
+
+    def remote(dst_rank, out_ap, in_ap, rsem, n):
+        dst = T.cores[dst_rank]
+        assert topo.may_write(core, dst)
+        rid, pid, _se = topo.addr(dst)
+        g.remote_dma(out_ap=out_ap, in_ap=in_ap, remote_sem=rsem, local_sem=sem.sent, pid=pid, routing_id=rid,
+                     dma_engine_mask=_engines(topo, core, dst, n))
+
+    if not mine:
+        h = HOST[rank]
+        j = rank - HOST.index(h)
+        g.wait_ge(sem.wl1, 16)
+        g.wait_ge(sem.wl2, 16)
+        remote(h, T.wts[:, j * WC:(j + 1) * WC], T.wts[:, 0:WC], sem["wr%d" % j], W_ENG)
+        g.wait_ge(sem.sent, W_ENG)
+        return
+
+    seen = {}
+
+    def wait(q, qn, sn, val):
+        if seen.get((qn, sn), 0) < val:
+            q.wait_ge(sem[sn], val)
+            seen[(qn, sn)] = val
+
+    k = len(mine)
+    last = mine[-1] == N - 1
+    need_in = 16 * BPC if rank == 0 else ACT_ENG
+    ve.memset(T.zero[:, :], 0.0).then_inc(sem.zs, 1)
+    ve.wait_ge(sem.zs, 1)
+
+    tasks = [(c, j) for c in range(NCH) for j in range(k)]
+    idx = dict((t, i) for i, t in enumerate(tasks))
+    for i, (c, j) in enumerate(tasks):
+        wb = j * WC
+        own = mine[j] == rank
+        if j == 0:
+            wait(te, "t", "arr%d" % c, need_in)
+            rhs = T.ain[:, c * CW:(c + 1) * CW]
+        else:
+            wait(te, "t", "vdone", 5 * idx[(c, j - 1)] + 5)
+            rhs = T.aout[:, (j - 1) * COLS + c * CW:(j - 1) * COLS + (c + 1) * CW]
+        if own:
+            wait(te, "t", "wl1", 16)
+        else:
+            wait(te, "t", "wr%d" % j, W_ENG)
+        for f in range(FT):
+            u = FT * i + f
+            if u >= NZ:
+                wait(te, "t", "vdone", 5 * ((u - NZ) // FT) + (u - NZ) % FT + 1)
+            te.matmul(T["z%d" % (u % NZ)][:, 0:CW], T.wts[:, wb + f * P:wb + (f + 1) * P], rhs,
+                      True, True).then_inc(sem.tdone, 1)
+        if own:
+            wait(te, "t", "wl2", 16)
+        acc = T["p%d" % (i % NA)][:, 0:CW]
+        for f in range(FT):
+            u = FT * i + f
+            wait(te, "t", "vdone", 5 * i + f + 1)
+            te.matmul(acc, T.wts[:, wb + (FT + f) * P:wb + (FT + f + 1) * P], T.hid[:, u * CW:(u + 1) * CW],
+                      f == 0, f == FT - 1).then_inc(sem.tdone, 1)
+        for f in range(FT):
+            u = FT * i + f
+            wait(ve, "v", "tdone", 8 * i + f + 1)
+            ve.tensor_tensor(T.hid[:, u * CW:(u + 1) * CW], T["z%d" % (u % NZ)][:, 0:CW], T.zero[:, :],
+                             AluOpType.max).then_inc(sem.vdone, 1)
+        wait(ve, "v", "tdone", 8 * i + 8)
+        ob = j * COLS + c * CW
+        ve.tensor_copy(T.aout[:, ob:ob + CW], acc).then_inc(sem.vdone, 1)
+        if j < k - 1:
+            continue
+        if last:
+            for b in range(BPC):
+                wait(ldq[b % 2], "q%d" % (b % 2), "vdone", 5 * i + 5)
+                ldq[b % 2].dma_start(T.y[c * BPC + b], T.aout[:, ob + b * TK:ob + (b + 1) * TK]).then_inc(
+                    sem["st%d" % b], 16)
+        else:
+            wait(g, "g", "vdone", 5 * i + 5)
+            remote(HOST[mine[-1] + 1], T.ain[:, c * CW:(c + 1) * CW], T.aout[:, ob:ob + CW], sem["arr%d" % c],
+                   ACT_ENG)
+    if last:
+        for b in range(BPC):
+            ldq[b % 2].wait_ge(sem["st%d" % b], 16 * NCH)
+    else:
+        g.wait_ge(sem.sent, ACT_ENG * NCH)

@@ -2,30 +2,35 @@ from concourse.mybir import AluOpType
 
 N, NB, TK, FT, P = 6, 4, 32, 4, 128
 HOST = [0, 1, 1, 5, 5, 5]
+SPLIT = {2: 2}
 NCH = 2
 COLS = NB * TK
 CW = COLS // NCH
 BPC = NB // NCH
 WC = 2 * FT * P
 MAXST = max(HOST.count(r) for r in range(N))
-NZ, NA = 6, 2
+RG = 2
+NR = FT // RG
 ACT_ENG = 8
 W_ENG = 8
+TPS = 2 * FT * NCH
+VPS = (NR + 1) * NCH
 
 SCRATCH = {
     "wts": ("sbuf", [P, MAXST * WC], "bfloat16"),
     "ain": ("sbuf", [P, COLS], "bfloat16"),
     "aout": ("sbuf", [P, MAXST * COLS], "bfloat16"),
     "hid": ("sbuf", [P, MAXST * NCH * FT * CW], "bfloat16"),
-    "zero": ("sbuf", [P, CW], "float32"),
+    "zero": ("sbuf", [P, RG * CW], "float32"),
 }
-for _i in range(NZ):
-    SCRATCH["z%d" % _i] = ("psum", [P, 512], "float32")
-for _i in range(NA):
-    SCRATCH["p%d" % _i] = ("psum", [P, 512], "float32")
+for _c in range(NCH):
+    for _r in range(NR):
+        SCRATCH["z%d_%d" % (_c, _r)] = ("psum", [P, 512], "float32")
+    SCRATCH["p%d" % _c] = ("psum", [P, 512], "float32")
 
 SEMAPHORES = (["wl1", "wl2", "zs", "tdone", "vdone", "sent"]
-              + ["arr%d" % c for c in range(NCH)] + ["wr%d" % j for j in range(MAXST)]
+              + ["arr%d" % c for c in range(NCH)]
+              + ["wr%d_%d" % (j, p) for j in range(MAXST) for p in range(2)]
               + ["st%d" % b for b in range(BPC)])
 
 
@@ -48,6 +53,7 @@ def rank_program(g, core, T, topo):
     ldq = [g.sync, g.scalar]
     mine = [s for s in range(N) if HOST[s] == rank]
     slot = (rank - mine[0]) if mine else 0
+    parts = SPLIT.get(rank, 1)
 
     def load_x(c):
         for b in range(BPC):
@@ -57,7 +63,8 @@ def rank_program(g, core, T, topo):
     if rank == 0:
         load_x(0)
     g.sync.dma_start(T.wts[:, slot * WC:slot * WC + FT * P], T.w1[:, :]).then_inc(sem.wl1, 16)
-    g.scalar.dma_start(T.wts[:, slot * WC + FT * P:(slot + 1) * WC], T.w2[:, :]).then_inc(sem.wl2, 16)
+    (g.sync if parts == 2 else g.scalar).dma_start(
+        T.wts[:, slot * WC + FT * P:(slot + 1) * WC], T.w2[:, :]).then_inc(sem.wl2, 16)
     if rank == 0:
         for c in range(1, NCH):
             load_x(c)
@@ -73,9 +80,14 @@ def rank_program(g, core, T, topo):
         h = HOST[rank]
         j = rank - HOST.index(h)
         g.wait_ge(sem.wl1, 16)
-        g.wait_ge(sem.wl2, 16)
-        remote(h, T.wts[:, j * WC:(j + 1) * WC], T.wts[:, 0:WC], sem["wr%d" % j], W_ENG)
-        g.wait_ge(sem.sent, W_ENG)
+        if parts == 2:
+            remote(h, T.wts[:, j * WC:j * WC + FT * P], T.wts[:, 0:FT * P], sem["wr%d_0" % j], W_ENG)
+            g.wait_ge(sem.wl2, 16)
+            remote(h, T.wts[:, j * WC + FT * P:(j + 1) * WC], T.wts[:, FT * P:WC], sem["wr%d_1" % j], W_ENG)
+        else:
+            g.wait_ge(sem.wl2, 16)
+            remote(h, T.wts[:, j * WC:(j + 1) * WC], T.wts[:, 0:WC], sem["wr%d_0" % j], W_ENG)
+        g.wait_ge(sem.sent, W_ENG * parts)
         return
 
     seen = {}
@@ -85,62 +97,75 @@ def rank_program(g, core, T, topo):
             q.wait_ge(sem[sn], val)
             seen[(qn, sn)] = val
 
+    def t_m1(j, c, f):
+        return TPS * j + FT * c + f + 1
+
+    def t_m2(j, c, f):
+        return TPS * j + FT * NCH + FT * c + f + 1
+
+    def v_r(j, c, r):
+        return VPS * j + NR * c + r + 1
+
+    def v_c(j, c):
+        return VPS * j + NR * NCH + c + 1
+
     k = len(mine)
     last = mine[-1] == N - 1
-    need_in = 16 * BPC if rank == 0 else ACT_ENG
     ve.memset(T.zero[:, :], 0.0).then_inc(sem.zs, 1)
     ve.wait_ge(sem.zs, 1)
 
-    tasks = [(c, j) for c in range(NCH) for j in range(k)]
-    idx = dict((t, i) for i, t in enumerate(tasks))
-    for i, (c, j) in enumerate(tasks):
+    for j in range(k):
         wb = j * WC
         own = mine[j] == rank
-        if j == 0:
-            wait(te, "t", "arr%d" % c, need_in)
-            rhs = T.ain[:, c * CW:(c + 1) * CW]
-        else:
-            wait(te, "t", "vdone", 5 * idx[(c, j - 1)] + 5)
-            rhs = T.aout[:, (j - 1) * COLS + c * CW:(j - 1) * COLS + (c + 1) * CW]
-        if own:
-            wait(te, "t", "wl1", 16)
-        else:
-            wait(te, "t", "wr%d" % j, W_ENG)
-        for f in range(FT):
-            u = FT * i + f
-            if u >= NZ:
-                wait(te, "t", "vdone", 5 * ((u - NZ) // FT) + (u - NZ) % FT + 1)
-            te.matmul(T["z%d" % (u % NZ)][:, 0:CW], T.wts[:, wb + f * P:wb + (f + 1) * P], rhs,
-                      True, True).then_inc(sem.tdone, 1)
+        for c in range(NCH):
+            if j > 0:
+                wait(te, "t", "vdone", v_c(j - 1, c))
+                rhs = T.aout[:, (j - 1) * COLS + c * CW:(j - 1) * COLS + (c + 1) * CW]
+            else:
+                if rank == 0:
+                    wait(te, "t", "arr%d" % c, 16 * BPC)
+                else:
+                    wait(te, "t", "arr0", ACT_ENG)
+                rhs = T.ain[:, c * CW:(c + 1) * CW]
+            if own:
+                wait(te, "t", "wl1", 16)
+            else:
+                wait(te, "t", "wr%d_0" % j, W_ENG)
+            for f in range(FT):
+                te.matmul(T["z%d_%d" % (c, f // RG)][:, (f % RG) * CW:(f % RG + 1) * CW],
+                          T.wts[:, wb + f * P:wb + (f + 1) * P], rhs, True, True).then_inc(sem.tdone, 1)
         if own:
             wait(te, "t", "wl2", 16)
-        acc = T["p%d" % (i % NA)][:, 0:CW]
-        for f in range(FT):
-            u = FT * i + f
-            wait(te, "t", "vdone", 5 * i + f + 1)
-            te.matmul(acc, T.wts[:, wb + (FT + f) * P:wb + (FT + f + 1) * P], T.hid[:, u * CW:(u + 1) * CW],
-                      f == 0, f == FT - 1).then_inc(sem.tdone, 1)
-        for f in range(FT):
-            u = FT * i + f
-            wait(ve, "v", "tdone", 8 * i + f + 1)
-            ve.tensor_tensor(T.hid[:, u * CW:(u + 1) * CW], T["z%d" % (u % NZ)][:, 0:CW], T.zero[:, :],
-                             AluOpType.max).then_inc(sem.vdone, 1)
-        wait(ve, "v", "tdone", 8 * i + 8)
-        ob = j * COLS + c * CW
-        ve.tensor_copy(T.aout[:, ob:ob + CW], acc).then_inc(sem.vdone, 1)
-        if j < k - 1:
-            continue
-        if last:
-            for b in range(BPC):
-                wait(ldq[b % 2], "q%d" % (b % 2), "vdone", 5 * i + 5)
-                ldq[b % 2].dma_start(T.y[c * BPC + b], T.aout[:, ob + b * TK:ob + (b + 1) * TK]).then_inc(
-                    sem["st%d" % b], 16)
-        else:
-            wait(g, "g", "vdone", 5 * i + 5)
-            remote(HOST[mine[-1] + 1], T.ain[:, c * CW:(c + 1) * CW], T.aout[:, ob:ob + CW], sem["arr%d" % c],
-                   ACT_ENG)
+        elif SPLIT.get(mine[j], 1) == 2:
+            wait(te, "t", "wr%d_1" % j, W_ENG)
+        for c in range(NCH):
+            hb = (j * NCH + c) * FT * CW
+            for f in range(FT):
+                wait(te, "t", "vdone", v_r(j, c, f // RG))
+                te.matmul(T["p%d" % c][:, 0:CW], T.wts[:, wb + (FT + f) * P:wb + (FT + f + 1) * P],
+                          T.hid[:, hb + f * CW:hb + (f + 1) * CW], f == 0, f == FT - 1).then_inc(sem.tdone, 1)
+        for c in range(NCH):
+            hb = (j * NCH + c) * FT * CW
+            for r in range(NR):
+                wait(ve, "v", "tdone", t_m1(j, c, r * RG + RG - 1))
+                ve.tensor_tensor(T.hid[:, hb + r * RG * CW:hb + (r + 1) * RG * CW],
+                                 T["z%d_%d" % (c, r)][:, 0:RG * CW], T.zero[:, :],
+                                 AluOpType.max).then_inc(sem.vdone, 1)
+        for c in range(NCH):
+            wait(ve, "v", "tdone", t_m2(j, c, FT - 1))
+            ob = j * COLS + c * CW
+            ve.tensor_copy(T.aout[:, ob:ob + CW], T["p%d" % c][:, 0:CW]).then_inc(sem.vdone, 1)
+
+    ob = (k - 1) * COLS
     if last:
+        for c in range(NCH):
+            for b in range(BPC):
+                m = c * BPC + b
+                wait(ldq[b % 2], "q%d" % (b % 2), "vdone", v_c(k - 1, c))
+                ldq[b % 2].dma_start(T.y[m], T.aout[:, ob + m * TK:ob + (m + 1) * TK]).then_inc(sem["st%d" % b], 16)
         for b in range(BPC):
             ldq[b % 2].wait_ge(sem["st%d" % b], 16 * NCH)
     else:
-        g.wait_ge(sem.sent, ACT_ENG * NCH)
+        wait(g, "g", "vdone", v_c(k - 1, NCH - 1))
+        remote(HOST[mine[-1] + 1], T.ain[:, :], T.aout[:, ob:ob + COLS], sem.arr0, ACT_ENG)
+        g.wait_ge(sem.sent, ACT_ENG)

@@ -2,31 +2,29 @@ from concourse.mybir import AluOpType
 
 N, NB, TK, FT, P = 6, 4, 32, 4, 128
 HOST = [0, 1, 1, 5, 5, 5]
-SPLIT = {2: 2}
+SPLIT = {2: 2, 3: 2, 4: 2}
 NCH = 2
 COLS = NB * TK
 CW = COLS // NCH
 BPC = NB // NCH
 WC = 2 * FT * P
 MAXST = max(HOST.count(r) for r in range(N))
-RG = 2
-NR = FT // RG
+ACC0 = 256
 ACT_ENG = 8
 W_ENG = 8
 TPS = 2 * FT * NCH
-VPS = (NR + 1) * NCH
+VPS = (FT + 1) * NCH
 
 SCRATCH = {
     "wts": ("sbuf", [P, MAXST * WC], "bfloat16"),
     "ain": ("sbuf", [P, COLS], "bfloat16"),
     "aout": ("sbuf", [P, MAXST * COLS], "bfloat16"),
     "hid": ("sbuf", [P, MAXST * NCH * FT * CW], "bfloat16"),
-    "zero": ("sbuf", [P, RG * CW], "float32"),
+    "zero": ("sbuf", [P, CW], "float32"),
 }
 for _c in range(NCH):
-    for _r in range(NR):
-        SCRATCH["z%d_%d" % (_c, _r)] = ("psum", [P, 512], "float32")
-    SCRATCH["p%d" % _c] = ("psum", [P, 512], "float32")
+    for _f in range(FT):
+        SCRATCH["z%d_%d" % (_c, _f)] = ("psum", [P, 512], "float32")
 
 SEMAPHORES = (["wl1", "wl2", "zs", "tdone", "vdone", "sent"]
               + ["arr%d" % c for c in range(NCH)]
@@ -55,19 +53,17 @@ def rank_program(g, core, T, topo):
     slot = (rank - mine[0]) if mine else 0
     parts = SPLIT.get(rank, 1)
 
-    def load_x(c):
+    def load_x(q, c):
         for b in range(BPC):
             m = c * BPC + b
-            ldq[b % 2].dma_start(T.ain[:, m * TK:(m + 1) * TK], T.x[m]).then_inc(sem["arr%d" % c], 16)
+            q.dma_start(T.ain[:, m * TK:(m + 1) * TK], T.x[m]).then_inc(sem["arr%d" % c], 16)
 
-    if rank == 0:
-        load_x(0)
     g.sync.dma_start(T.wts[:, slot * WC:slot * WC + FT * P], T.w1[:, :]).then_inc(sem.wl1, 16)
+    if rank == 0:
+        load_x(g.scalar, 0)
+        load_x(g.sync, 1)
     (g.sync if parts == 2 else g.scalar).dma_start(
         T.wts[:, slot * WC + FT * P:(slot + 1) * WC], T.w2[:, :]).then_inc(sem.wl2, 16)
-    if rank == 0:
-        for c in range(1, NCH):
-            load_x(c)
 
     def remote(dst_rank, out_ap, in_ap, rsem, n):
         dst = T.cores[dst_rank]
@@ -103,14 +99,15 @@ def rank_program(g, core, T, topo):
     def t_m2(j, c, f):
         return TPS * j + FT * NCH + FT * c + f + 1
 
-    def v_r(j, c, r):
-        return VPS * j + NR * c + r + 1
+    def v_r(j, c, f):
+        return VPS * j + FT * c + f + 1
 
     def v_c(j, c):
-        return VPS * j + NR * NCH + c + 1
+        return VPS * j + FT * NCH + c + 1
 
     k = len(mine)
     last = mine[-1] == N - 1
+    need_in = 16 * BPC if rank == 0 else ACT_ENG
     ve.memset(T.zero[:, :], 0.0).then_inc(sem.zs, 1)
     ve.wait_ge(sem.zs, 1)
 
@@ -122,18 +119,15 @@ def rank_program(g, core, T, topo):
                 wait(te, "t", "vdone", v_c(j - 1, c))
                 rhs = T.aout[:, (j - 1) * COLS + c * CW:(j - 1) * COLS + (c + 1) * CW]
             else:
-                if rank == 0:
-                    wait(te, "t", "arr%d" % c, 16 * BPC)
-                else:
-                    wait(te, "t", "arr0", ACT_ENG)
+                wait(te, "t", "arr%d" % c, need_in)
                 rhs = T.ain[:, c * CW:(c + 1) * CW]
             if own:
                 wait(te, "t", "wl1", 16)
             else:
                 wait(te, "t", "wr%d_0" % j, W_ENG)
             for f in range(FT):
-                te.matmul(T["z%d_%d" % (c, f // RG)][:, (f % RG) * CW:(f % RG + 1) * CW],
-                          T.wts[:, wb + f * P:wb + (f + 1) * P], rhs, True, True).then_inc(sem.tdone, 1)
+                te.matmul(T["z%d_%d" % (c, f)][:, 0:CW], T.wts[:, wb + f * P:wb + (f + 1) * P], rhs,
+                          True, True).then_inc(sem.tdone, 1)
         if own:
             wait(te, "t", "wl2", 16)
         elif SPLIT.get(mine[j], 1) == 2:
@@ -141,20 +135,19 @@ def rank_program(g, core, T, topo):
         for c in range(NCH):
             hb = (j * NCH + c) * FT * CW
             for f in range(FT):
-                wait(te, "t", "vdone", v_r(j, c, f // RG))
-                te.matmul(T["p%d" % c][:, 0:CW], T.wts[:, wb + (FT + f) * P:wb + (FT + f + 1) * P],
+                wait(te, "t", "vdone", v_r(j, c, f))
+                te.matmul(T["z%d_0" % c][:, ACC0:ACC0 + CW], T.wts[:, wb + (FT + f) * P:wb + (FT + f + 1) * P],
                           T.hid[:, hb + f * CW:hb + (f + 1) * CW], f == 0, f == FT - 1).then_inc(sem.tdone, 1)
         for c in range(NCH):
             hb = (j * NCH + c) * FT * CW
-            for r in range(NR):
-                wait(ve, "v", "tdone", t_m1(j, c, r * RG + RG - 1))
-                ve.tensor_tensor(T.hid[:, hb + r * RG * CW:hb + (r + 1) * RG * CW],
-                                 T["z%d_%d" % (c, r)][:, 0:RG * CW], T.zero[:, :],
-                                 AluOpType.max).then_inc(sem.vdone, 1)
+            for f in range(FT):
+                wait(ve, "v", "tdone", t_m1(j, c, f))
+                ve.tensor_tensor(T.hid[:, hb + f * CW:hb + (f + 1) * CW], T["z%d_%d" % (c, f)][:, 0:CW],
+                                 T.zero[:, :], AluOpType.max).then_inc(sem.vdone, 1)
         for c in range(NCH):
             wait(ve, "v", "tdone", t_m2(j, c, FT - 1))
             ob = j * COLS + c * CW
-            ve.tensor_copy(T.aout[:, ob:ob + CW], T["p%d" % c][:, 0:CW]).then_inc(sem.vdone, 1)
+            ve.tensor_copy(T.aout[:, ob:ob + CW], T["z%d_0" % c][:, ACC0:ACC0 + CW]).then_inc(sem.vdone, 1)
 
     ob = (k - 1) * COLS
     if last:
@@ -166,6 +159,8 @@ def rank_program(g, core, T, topo):
         for b in range(BPC):
             ldq[b % 2].wait_ge(sem["st%d" % b], 16 * NCH)
     else:
-        wait(g, "g", "vdone", v_c(k - 1, NCH - 1))
-        remote(HOST[mine[-1] + 1], T.ain[:, :], T.aout[:, ob:ob + COLS], sem.arr0, ACT_ENG)
-        g.wait_ge(sem.sent, ACT_ENG)
+        for c in range(NCH):
+            wait(g, "g", "vdone", v_c(k - 1, c))
+            remote(HOST[mine[-1] + 1], T.ain[:, c * CW:(c + 1) * CW], T.aout[:, ob + c * CW:ob + (c + 1) * CW],
+                   sem["arr%d" % c], ACT_ENG)
+        g.wait_ge(sem.sent, ACT_ENG * NCH)

@@ -1,19 +1,18 @@
 from concourse.mybir import AluOpType
 
 N, NB, TK, FT, P = 6, 4, 32, 4, 128
-HOST = [0, 1, 1, 5, 5, 5]
-SPLIT = {2: 2, 3: 2, 4: 2}
 NCH = 2
+PLACE = [[0, 0], [1, 2], [1, 2], [5, 5], [5, 5], [5, 5]]
+RELAY = {(4, 1)}
 COLS = NB * TK
 CW = COLS // NCH
 BPC = NB // NCH
 WC = 2 * FT * P
-MAXST = max(HOST.count(r) for r in range(N))
+MAPS = [[s for s in range(N) if r in PLACE[s]] for r in range(N)]
+MAXST = max(len(m) for m in MAPS)
 ACC0 = 256
 ACT_ENG = 8
 W_ENG = 8
-TPS = 2 * FT * NCH
-VPS = (FT + 1) * NCH
 
 SCRATCH = {
     "wts": ("sbuf", [P, MAXST * WC], "bfloat16"),
@@ -26,7 +25,7 @@ for _c in range(NCH):
     for _f in range(FT):
         SCRATCH["z%d_%d" % (_c, _f)] = ("psum", [P, 512], "float32")
 
-SEMAPHORES = (["wl1", "wl2", "zs", "tdone", "vdone", "sent"]
+SEMAPHORES = (["wl1", "wl2", "zs", "tdone", "vdone", "sent", "rly"]
               + ["arr%d" % c for c in range(NCH)]
               + ["wr%d_%d" % (j, p) for j in range(MAXST) for p in range(2)]
               + ["st%d" % b for b in range(BPC)])
@@ -42,68 +41,110 @@ def _engines(topo, src, dst, n):
     return m
 
 
+def _count(m):
+    return bin(m).count("1")
+
+
+def _helper(topo, T, src, dst):
+    for c in range(topo.CHIPS * topo.CORES_PER_CHIP):
+        if (topo.chip(c) == topo.chip(src) and topo.die(c) != topo.die(src) and T.rank_of(c) is None
+                and topo.may_write(c, dst)):
+            return c
+    return None
+
+
+def _dests(r):
+    return sorted(set(h for h in PLACE[r] if h != r))
+
+
 def rank_program(g, core, T, topo):
     rank = T.rank_of(core)
-    if rank is None:
-        return
     sem = T.sem
+    nsent = [0]
+
+    def remote(dst, out_ap, in_ap, rsem, n):
+        assert topo.may_write(core, dst)
+        rid, pid, _se = topo.addr(dst)
+        g.remote_dma(out_ap=out_ap, in_ap=in_ap, remote_sem=rsem, local_sem=sem.sent, pid=pid, routing_id=rid,
+                     dma_engine_mask=_engines(topo, core, dst, n))
+        nsent[0] += n
+
+    if rank is None:
+        for r, p in sorted(RELAY):
+            for h in _dests(r):
+                if _helper(topo, T, T.cores[r], T.cores[h]) == core:
+                    j = r - MAPS[h][0]
+                    g.wait_ge(sem.rly, _count(topo.mask(T.cores[r], core)))
+                    remote(T.cores[h], T.wts[:, j * WC + p * FT * P:j * WC + (p + 1) * FT * P], T.wts[:, 0:FT * P],
+                           sem["wr%d_%d" % (j, p)], W_ENG)
+                    g.wait_ge(sem.sent, nsent[0])
+        return
     te, ve = g.tensor, g.vector
     ldq = [g.sync, g.scalar]
-    mine = [s for s in range(N) if HOST[s] == rank]
-    slot = (rank - mine[0]) if mine else 0
-    parts = SPLIT.get(rank, 1)
+    mine = MAPS[rank]
+    chs = [c for c in range(NCH) if PLACE[mine[0]][c] == rank] if mine else []
+    nl = len(chs)
+    slot = (rank - mine[0]) if rank in mine else 0
+    dests = _dests(rank)
+    parts = sorted(range(2), key=lambda p: (rank, p) not in RELAY)
 
     def load_x(q, c):
         for b in range(BPC):
             m = c * BPC + b
             q.dma_start(T.ain[:, m * TK:(m + 1) * TK], T.x[m]).then_inc(sem["arr%d" % c], 16)
 
-    g.sync.dma_start(T.wts[:, slot * WC:slot * WC + FT * P], T.w1[:, :]).then_inc(sem.wl1, 16)
+    def load_w(q, p):
+        q.dma_start(T.wts[:, slot * WC + p * FT * P:slot * WC + (p + 1) * FT * P],
+                    (T.w1, T.w2)[p][:, :]).then_inc(sem[("wl1", "wl2")[p]], 16)
+
     if rank == 0:
+        load_w(g.sync, 0)
         load_x(g.scalar, 0)
         load_x(g.sync, 1)
-    (g.sync if parts == 2 else g.scalar).dma_start(
-        T.wts[:, slot * WC + FT * P:(slot + 1) * WC], T.w2[:, :]).then_inc(sem.wl2, 16)
+        load_w(g.scalar, 1)
+    elif dests:
+        for p in parts:
+            load_w(g.sync, p)
+    else:
+        load_w(g.sync, 0)
+        load_w(g.scalar, 1)
 
-    def remote(dst_rank, out_ap, in_ap, rsem, n):
-        dst = T.cores[dst_rank]
-        assert topo.may_write(core, dst)
-        rid, pid, _se = topo.addr(dst)
-        g.remote_dma(out_ap=out_ap, in_ap=in_ap, remote_sem=rsem, local_sem=sem.sent, pid=pid, routing_id=rid,
-                     dma_engine_mask=_engines(topo, core, dst, n))
-
+    for p in parts:
+        if dests:
+            g.wait_ge(sem[("wl1", "wl2")[p]], 16)
+        for h in dests:
+            j = rank - MAPS[h][0]
+            src_ap = T.wts[:, slot * WC + p * FT * P:slot * WC + (p + 1) * FT * P]
+            if (rank, p) in RELAY:
+                hc = _helper(topo, T, core, T.cores[h])
+                remote(hc, T.wts[:, 0:FT * P], src_ap, sem.rly, _count(topo.mask(core, hc)))
+            else:
+                remote(T.cores[h], T.wts[:, j * WC + p * FT * P:j * WC + (p + 1) * FT * P], src_ap,
+                       sem["wr%d_%d" % (j, p)], W_ENG)
     if not mine:
-        h = HOST[rank]
-        j = rank - HOST.index(h)
-        g.wait_ge(sem.wl1, 16)
-        if parts == 2:
-            remote(h, T.wts[:, j * WC:j * WC + FT * P], T.wts[:, 0:FT * P], sem["wr%d_0" % j], W_ENG)
-            g.wait_ge(sem.wl2, 16)
-            remote(h, T.wts[:, j * WC + FT * P:(j + 1) * WC], T.wts[:, FT * P:WC], sem["wr%d_1" % j], W_ENG)
-        else:
-            g.wait_ge(sem.wl2, 16)
-            remote(h, T.wts[:, j * WC:(j + 1) * WC], T.wts[:, 0:WC], sem["wr%d_0" % j], W_ENG)
-        g.wait_ge(sem.sent, W_ENG * parts)
+        g.wait_ge(sem.sent, nsent[0])
         return
 
     seen = {}
+    TPS = 2 * FT * nl
+    VPS = (FT + 1) * nl
 
     def wait(q, qn, sn, val):
         if seen.get((qn, sn), 0) < val:
             q.wait_ge(sem[sn], val)
             seen[(qn, sn)] = val
 
-    def t_m1(j, c, f):
-        return TPS * j + FT * c + f + 1
+    def t_m1(j, i, f):
+        return TPS * j + FT * i + f + 1
 
-    def t_m2(j, c, f):
-        return TPS * j + FT * NCH + FT * c + f + 1
+    def t_m2(j, i, f):
+        return TPS * j + FT * nl + FT * i + f + 1
 
-    def v_r(j, c, f):
-        return VPS * j + FT * c + f + 1
+    def v_r(j, i, f):
+        return VPS * j + FT * i + f + 1
 
-    def v_c(j, c):
-        return VPS * j + FT * NCH + c + 1
+    def v_c(j, i):
+        return VPS * j + FT * nl + i + 1
 
     k = len(mine)
     last = mine[-1] == N - 1
@@ -114,9 +155,9 @@ def rank_program(g, core, T, topo):
     for j in range(k):
         wb = j * WC
         own = mine[j] == rank
-        for c in range(NCH):
+        for i, c in enumerate(chs):
             if j > 0:
-                wait(te, "t", "vdone", v_c(j - 1, c))
+                wait(te, "t", "vdone", v_c(j - 1, i))
                 rhs = T.aout[:, (j - 1) * COLS + c * CW:(j - 1) * COLS + (c + 1) * CW]
             else:
                 wait(te, "t", "arr%d" % c, need_in)
@@ -130,37 +171,37 @@ def rank_program(g, core, T, topo):
                           True, True).then_inc(sem.tdone, 1)
         if own:
             wait(te, "t", "wl2", 16)
-        elif SPLIT.get(mine[j], 1) == 2:
+        else:
             wait(te, "t", "wr%d_1" % j, W_ENG)
-        for c in range(NCH):
-            hb = (j * NCH + c) * FT * CW
+        for i, c in enumerate(chs):
+            hb = (j * nl + i) * FT * CW
             for f in range(FT):
-                wait(te, "t", "vdone", v_r(j, c, f))
+                wait(te, "t", "vdone", v_r(j, i, f))
                 te.matmul(T["z%d_0" % c][:, ACC0:ACC0 + CW], T.wts[:, wb + (FT + f) * P:wb + (FT + f + 1) * P],
                           T.hid[:, hb + f * CW:hb + (f + 1) * CW], f == 0, f == FT - 1).then_inc(sem.tdone, 1)
-        for c in range(NCH):
-            hb = (j * NCH + c) * FT * CW
+        for i, c in enumerate(chs):
+            hb = (j * nl + i) * FT * CW
             for f in range(FT):
-                wait(ve, "v", "tdone", t_m1(j, c, f))
+                wait(ve, "v", "tdone", t_m1(j, i, f))
                 ve.tensor_tensor(T.hid[:, hb + f * CW:hb + (f + 1) * CW], T["z%d_%d" % (c, f)][:, 0:CW],
                                  T.zero[:, :], AluOpType.max).then_inc(sem.vdone, 1)
-        for c in range(NCH):
-            wait(ve, "v", "tdone", t_m2(j, c, FT - 1))
+        for i, c in enumerate(chs):
+            wait(ve, "v", "tdone", t_m2(j, i, FT - 1))
             ob = j * COLS + c * CW
             ve.tensor_copy(T.aout[:, ob:ob + CW], T["z%d_0" % c][:, ACC0:ACC0 + CW]).then_inc(sem.vdone, 1)
 
     ob = (k - 1) * COLS
     if last:
-        for c in range(NCH):
+        for i, c in enumerate(chs):
             for b in range(BPC):
                 m = c * BPC + b
-                wait(ldq[b % 2], "q%d" % (b % 2), "vdone", v_c(k - 1, c))
+                wait(ldq[b % 2], "q%d" % (b % 2), "vdone", v_c(k - 1, i))
                 ldq[b % 2].dma_start(T.y[m], T.aout[:, ob + m * TK:ob + (m + 1) * TK]).then_inc(sem["st%d" % b], 16)
         for b in range(BPC):
-            ldq[b % 2].wait_ge(sem["st%d" % b], 16 * NCH)
+            ldq[b % 2].wait_ge(sem["st%d" % b], 16 * nl)
     else:
-        for c in range(NCH):
-            wait(g, "g", "vdone", v_c(k - 1, c))
-            remote(HOST[mine[-1] + 1], T.ain[:, c * CW:(c + 1) * CW], T.aout[:, ob + c * CW:ob + (c + 1) * CW],
-                   sem["arr%d" % c], ACT_ENG)
-        g.wait_ge(sem.sent, ACT_ENG * NCH)
+        for i, c in enumerate(chs):
+            wait(g, "g", "vdone", v_c(k - 1, i))
+            remote(T.cores[PLACE[mine[-1] + 1][c]], T.ain[:, c * CW:(c + 1) * CW],
+                   T.aout[:, ob + c * CW:ob + (c + 1) * CW], sem["arr%d" % c], ACT_ENG)
+        g.wait_ge(sem.sent, nsent[0])

from concourse.mybir import AluOpType

N, NB, TK, FT, P = 6, 4, 32, 4, 128
NCH = 2
PLACE = [[0, 0], [1, 2], [1, 2], [5, 5], [5, 5], [5, 5]]
RELAY = {(4, 1)}
COLS = NB * TK
CW = COLS // NCH
BPC = NB // NCH
WC = 2 * FT * P
MAPS = [[s for s in range(N) if r in PLACE[s]] for r in range(N)]
MAXST = max(len(m) for m in MAPS)
ACC0 = 256
ACT_ENG = 8
W_ENG = 8

SCRATCH = {
    "wts": ("sbuf", [P, MAXST * WC], "bfloat16"),
    "ain": ("sbuf", [P, COLS], "bfloat16"),
    "aout": ("sbuf", [P, MAXST * COLS], "bfloat16"),
    "hid": ("sbuf", [P, MAXST * NCH * FT * CW], "bfloat16"),
    "zero": ("sbuf", [P, CW], "float32"),
}
for _c in range(NCH):
    for _f in range(FT):
        SCRATCH["z%d_%d" % (_c, _f)] = ("psum", [P, 512], "float32")

SEMAPHORES = (["wl1", "wl2", "zs", "tdone", "vdone", "sent", "rly"]
              + ["arr%d" % c for c in range(NCH)]
              + ["wr%d_%d" % (j, p) for j in range(MAXST) for p in range(2)]
              + ["st%d" % b for b in range(BPC)])


def _engines(topo, src, dst, n):
    full, m, b, k = topo.mask(src, dst), 0, 0, 0
    while k < n:
        if (full >> b) & 1:
            m |= 1 << b
            k += 1
        b += 1
    return m


def _count(m):
    return bin(m).count("1")


def _helper(topo, T, src, dst):
    for c in range(topo.CHIPS * topo.CORES_PER_CHIP):
        if (topo.chip(c) == topo.chip(src) and topo.die(c) != topo.die(src) and T.rank_of(c) is None
                and topo.may_write(c, dst)):
            return c
    return None


def _dests(r):
    return sorted(set(h for h in PLACE[r] if h != r))


def rank_program(g, core, T, topo):
    rank = T.rank_of(core)
    sem = T.sem
    nsent = [0]

    def remote(dst, out_ap, in_ap, rsem, n):
        assert topo.may_write(core, dst)
        rid, pid, _se = topo.addr(dst)
        g.remote_dma(out_ap=out_ap, in_ap=in_ap, remote_sem=rsem, local_sem=sem.sent, pid=pid, routing_id=rid,
                     dma_engine_mask=_engines(topo, core, dst, n))
        nsent[0] += n

    if rank is None:
        for r, p in sorted(RELAY):
            for h in _dests(r):
                if _helper(topo, T, T.cores[r], T.cores[h]) == core:
                    j = r - MAPS[h][0]
                    g.wait_ge(sem.rly, _count(topo.mask(T.cores[r], core)))
                    remote(T.cores[h], T.wts[:, j * WC + p * FT * P:j * WC + (p + 1) * FT * P], T.wts[:, 0:FT * P],
                           sem["wr%d_%d" % (j, p)], W_ENG)
                    g.wait_ge(sem.sent, nsent[0])
        return
    te, ve = g.tensor, g.vector
    ldq = [g.sync, g.scalar]
    mine = MAPS[rank]
    chs = [c for c in range(NCH) if PLACE[mine[0]][c] == rank] if mine else []
    nl = len(chs)
    slot = (rank - mine[0]) if rank in mine else 0
    dests = _dests(rank)
    parts = sorted(range(2), key=lambda p: (rank, p) not in RELAY)

    def load_x(q, c):
        for b in range(BPC):
            m = c * BPC + b
            q.dma_start(T.ain[:, m * TK:(m + 1) * TK], T.x[m]).then_inc(sem["arr%d" % c], 16)

    def load_w(q, p):
        q.dma_start(T.wts[:, slot * WC + p * FT * P:slot * WC + (p + 1) * FT * P],
                    (T.w1, T.w2)[p][:, :]).then_inc(sem[("wl1", "wl2")[p]], 16)

    if rank == 0:
        load_w(g.sync, 0)
        load_x(g.scalar, 0)
        load_x(g.sync, 1)
        load_w(g.scalar, 1)
    elif dests:
        for p in parts:
            load_w(g.sync, p)
    else:
        load_w(g.sync, 0)
        load_w(g.scalar, 1)

    for p in parts:
        if dests:
            g.wait_ge(sem[("wl1", "wl2")[p]], 16)
        for h in dests:
            j = rank - MAPS[h][0]
            src_ap = T.wts[:, slot * WC + p * FT * P:slot * WC + (p + 1) * FT * P]
            if (rank, p) in RELAY:
                hc = _helper(topo, T, core, T.cores[h])
                remote(hc, T.wts[:, 0:FT * P], src_ap, sem.rly, _count(topo.mask(core, hc)))
            else:
                remote(T.cores[h], T.wts[:, j * WC + p * FT * P:j * WC + (p + 1) * FT * P], src_ap,
                       sem["wr%d_%d" % (j, p)], W_ENG)
    if not mine:
        g.wait_ge(sem.sent, nsent[0])
        return

    seen = {}
    TPS = 2 * FT * nl
    VPS = (FT + 1) * nl

    def wait(q, qn, sn, val):
        if seen.get((qn, sn), 0) < val:
            q.wait_ge(sem[sn], val)
            seen[(qn, sn)] = val

    def t_m1(j, i, f):
        return TPS * j + FT * i + f + 1

    def t_m2(j, i, f):
        return TPS * j + FT * nl + FT * i + f + 1

    def v_r(j, i, f):
        return VPS * j + FT * i + f + 1

    def v_c(j, i):
        return VPS * j + FT * nl + i + 1

    k = len(mine)
    last = mine[-1] == N - 1
    need_in = 16 * BPC if rank == 0 else ACT_ENG
    ve.memset(T.zero[:, :], 0.0).then_inc(sem.zs, 1)
    ve.wait_ge(sem.zs, 1)

    for j in range(k):
        wb = j * WC
        own = mine[j] == rank
        for i, c in enumerate(chs):
            if j > 0:
                wait(te, "t", "vdone", v_c(j - 1, i))
                rhs = T.aout[:, (j - 1) * COLS + c * CW:(j - 1) * COLS + (c + 1) * CW]
            else:
                wait(te, "t", "arr%d" % c, need_in)
                rhs = T.ain[:, c * CW:(c + 1) * CW]
            if own:
                wait(te, "t", "wl1", 16)
            else:
                wait(te, "t", "wr%d_0" % j, W_ENG)
            for f in range(FT):
                te.matmul(T["z%d_%d" % (c, f)][:, 0:CW], T.wts[:, wb + f * P:wb + (f + 1) * P], rhs,
                          True, True).then_inc(sem.tdone, 1)
        if own:
            wait(te, "t", "wl2", 16)
        else:
            wait(te, "t", "wr%d_1" % j, W_ENG)
        for i, c in enumerate(chs):
            hb = (j * nl + i) * FT * CW
            for f in range(FT):
                wait(te, "t", "vdone", v_r(j, i, f))
                te.matmul(T["z%d_0" % c][:, ACC0:ACC0 + CW], T.wts[:, wb + (FT + f) * P:wb + (FT + f + 1) * P],
                          T.hid[:, hb + f * CW:hb + (f + 1) * CW], f == 0, f == FT - 1).then_inc(sem.tdone, 1)
        for i, c in enumerate(chs):
            hb = (j * nl + i) * FT * CW
            for f in range(FT):
                wait(ve, "v", "tdone", t_m1(j, i, f))
                ve.tensor_tensor(T.hid[:, hb + f * CW:hb + (f + 1) * CW], T["z%d_%d" % (c, f)][:, 0:CW],
                                 T.zero[:, :], AluOpType.max).then_inc(sem.vdone, 1)
        for i, c in enumerate(chs):
            wait(ve, "v", "tdone", t_m2(j, i, FT - 1))
            ob = j * COLS + c * CW
            ve.tensor_copy(T.aout[:, ob:ob + CW], T["z%d_0" % c][:, ACC0:ACC0 + CW]).then_inc(sem.vdone, 1)

    ob = (k - 1) * COLS
    if last:
        for i, c in enumerate(chs):
            for b in range(BPC):
                m = c * BPC + b
                wait(ldq[b % 2], "q%d" % (b % 2), "vdone", v_c(k - 1, i))
                ldq[b % 2].dma_start(T.y[m], T.aout[:, ob + m * TK:ob + (m + 1) * TK]).then_inc(sem["st%d" % b], 16)
        for b in range(BPC):
            ldq[b % 2].wait_ge(sem["st%d" % b], 16 * nl)
    else:
        for i, c in enumerate(chs):
            wait(g, "g", "vdone", v_c(k - 1, i))
            remote(T.cores[PLACE[mine[-1] + 1][c]], T.ain[:, c * CW:(c + 1) * CW],
                   T.aout[:, ob + c * CW:ob + (c + 1) * CW], sem["arr%d" % c], ACT_ENG)
        g.wait_ge(sem.sent, nsent[0])
